import numpy as np
import ml_dtypes


def mxq(x, axis, fmt="e4m3"):
    dtype, down = {"e4m3": (ml_dtypes.float8_e4m3fn, 7), "e5m2": (ml_dtypes.float8_e5m2, 14)}[fmt]
    v = np.moveaxis(np.asarray(x, np.float32).astype(ml_dtypes.bfloat16).astype(np.float64), axis, -1)
    blocks = v.reshape(v.shape[:-1] + (-1, 32))
    amax = np.abs(blocks).max(-1, keepdims=True)
    byte = np.maximum(np.where(amax > 0, np.frexp(amax)[1] - 1 + 127, 0) - down, 1)
    scale = np.exp2(byte - 127.0)
    codes = (blocks / scale).astype(np.float32).astype(dtype).astype(np.float64)
    return np.moveaxis((codes * scale).reshape(v.shape), -1, axis)


WIDE = False


def mx_kscale(k):
    if not WIDE:
        return np.ones(k)
    levels = np.array([10, -10, 5, -5, 0])
    if k % 512:
        return np.exp2(np.random.permutation(np.resize(levels, k // 32))).repeat(32)
    a = np.empty((k // 512, 16))
    for p in range(k // 512):
        a[p, :8] = np.random.permutation(np.resize(levels, 8))
        for g in range(8):
            far = levels[np.abs(levels - a[p, g]) >= 10]
            a[p, g + 8] = far[np.random.randint(len(far))]
    return np.exp2(a.ravel()).repeat(32)


def f64(x):
    return np.asarray(x).astype(np.float64)


def striped(idx):
    return np.tile(idx.reshape(-1, 16).T, (8, 1)).astype(np.uint16)


def unstriped(offs):
    return offs[:16].T.reshape(-1).astype(np.int64)


def striped8(idx):
    return np.concatenate([x.reshape(-1, 16).T for x in idx]).astype(np.uint16)


def runs(offs, k):
    lists = np.stack([offs[16 * r : 16 * r + 16].T.reshape(-1) for r in range(8)]).astype(np.int64)
    return lists[np.arange(k) % 512 // 64]


def pack_weight(w):
    k, n = w.shape
    w = f64(np.asarray(w, np.float32).astype(ml_dtypes.bfloat16)).reshape(k // 32, 32, n)
    amax = np.abs(w).max(1)
    byte = np.clip(np.where(amax > 0, np.frexp(amax)[1] - 1 + 127 - 7, 1), 1, 254)
    scaled = (w * np.exp2(127.0 - byte)[:, None, :]).reshape(k, n).astype(np.float32)
    words = np.ascontiguousarray(scaled.reshape(k // 512, 128, 4, n).transpose(0, 1, 3, 2)).astype(ml_dtypes.float8_e4m3fn).view(np.uint8)
    return words, np.ascontiguousarray(byte.astype(np.uint8).reshape(k // 512, 16, n))


def unpack_weight(words, scales):
    g, p, n, _ = words.shape
    vals = np.ascontiguousarray(words).view(ml_dtypes.float8_e4m3fn).astype(np.float64) * np.repeat(np.exp2(scales.astype(np.float64) - 127.0), 8, axis=1)[..., None]
    return vals.transpose(0, 1, 3, 2).reshape(g * 512, n)


E2M1 = np.array([0.0, 0.5, 1.0, 1.5, 2.0, 3.0, 4.0, 6.0, -0.0, -0.5, -1.0, -1.5, -2.0, -3.0, -4.0, -6.0])


def pack_fp4(w):
    k, n = w.shape
    w = f64(np.asarray(w, np.float32).astype(ml_dtypes.bfloat16)).reshape(k // 32, 32, n)
    amax = np.abs(w).max(1)
    mant, ex = np.frexp(amax / 6.0)
    byte = np.clip(np.where(amax > 0, np.where(mant > 0.5, ex, ex - 1) + 127, 1), 1, 254)
    scaled = (w * np.exp2(127.0 - byte)[:, None, :]).reshape(k, n).astype(np.float32)
    c = np.ascontiguousarray(scaled.reshape(k // 512, 128, 4, n).transpose(0, 1, 3, 2)).astype(ml_dtypes.float4_e2m1fn).view(np.uint8) & 0xF
    words = (c[..., 0::2] | (c[..., 1::2] << 4)).reshape(k // 512, 128, 2 * n)
    return np.ascontiguousarray(words), np.ascontiguousarray(byte.astype(np.uint8).reshape(k // 512, 16, n))


def unpack_fp4(words, scales):
    g, _, n = scales.shape
    words = np.ascontiguousarray(words).reshape(g, 128, n, 2)
    nib = np.empty((g, 128, n, 4), np.uint8)
    nib[..., 0::2] = words & 0xF
    nib[..., 1::2] = words >> 4
    vals = E2M1[nib] * np.repeat(np.exp2(scales.astype(np.float64) - 127.0), 8, axis=1)[..., None]
    return vals.transpose(0, 1, 3, 2).reshape(g * 512, n)


def sigmoid(v):
    return 1.0 / (1.0 + np.exp(-np.maximum(v, -700.0)))

def planes(y):
    n, m = y.shape
    v = y.astype(np.float32).astype(ml_dtypes.bfloat16).astype(np.float64).reshape(n // 32, 32, m)
    top = np.abs(v).max(1)
    byte = np.clip(np.where(top > 0, np.frexp(top)[1] - 1 + 127 - 7, 1), 1, 254)
    codes = (v * np.exp2(127.0 - byte)[:, None, :]).reshape(n, m).astype(np.float32).astype(ml_dtypes.float8_e4m3fn).view(np.uint8)
    words = codes.reshape(n // 512, 128, 4, m).transpose(0, 1, 3, 2)
    return np.ascontiguousarray(words), np.ascontiguousarray(byte.astype(np.uint8).reshape(n // 512, 16, m))


K, T, S, N, H = 512, 2048, 512, 512, 512


def setup_inputs():
    n = np.random.standard_normal
    s = mx_kscale(K)[:, None]
    u = mx_kscale(H)
    packed_xT = pack_weight(n((K, T)) * s)
    packed_w1 = pack_fp4(n((K, H)) / np.sqrt(K) / s)
    packed_w2 = pack_fp4(n((K, H)) / np.sqrt(K) / s)
    packed_w3 = pack_fp4(n((K, H)) / np.sqrt(K) / s)
    packed_w4 = pack_fp4(n((H, N)) / np.sqrt(H) / u[:, None])
    return {
        "x_words": packed_xT[0],
        "x_scales": packed_xT[1],
        "w1_words": packed_w1[0],
        "w1_scales": packed_w1[1],
        "w2_words": packed_w2[0],
        "w2_scales": packed_w2[1],
        "w3_words": packed_w3[0],
        "w3_scales": packed_w3[1],
        "gn": (np.random.uniform(0.5, 1.5, (H, 1)) * u[:, None]).astype(np.float32),
        "w4_words": packed_w4[0],
        "w4_scales": packed_w4[1],
        "offs": striped(np.random.permutation(T)[:S]),
        "two": striped(np.random.permutation(T)[:S]),
        "thr": striped(np.random.permutation(T)[:S]),
        "q1": striped8(np.stack([np.random.permutation(S) for _ in range(8)])),
        "q2": striped8(np.stack([np.random.permutation(S) for _ in range(8)])),
        "q3": striped8(np.stack([np.random.permutation(S) for _ in range(8)])),
        "q4": striped8(np.stack([np.random.permutation(S) for _ in range(8)])),
    }


def reference(x_words, x_scales, w1_words, w1_scales, w2_words, w2_scales, w3_words, w3_scales, gn, w4_words, w4_scales, offs, two, thr, q1, q2, q3, q4):
    xq = unpack_weight(x_words, x_scales)[:, unstriped(offs)]
    y = unpack_fp4(w1_words, w1_scales).T @ xq
    x_two = unpack_weight(x_words, x_scales)[:, unstriped(two)]
    fx = sigmoid(unpack_fp4(w2_words, w2_scales).T @ x_two)
    top = y[np.arange(H)[:, None], runs(q1, H)] + fx * (y[np.arange(H)[:, None], runs(q2, H)] - (y[np.arange(H)[:, None], runs(q1, H)]))
    x_thr = unpack_weight(x_words, x_scales)[:, unstriped(thr)]
    fy = sigmoid(unpack_fp4(w3_words, w3_scales).T @ x_thr)
    bot = y[np.arange(H)[:, None], runs(q3, H)] + fx * (y[np.arange(H)[:, None], runs(q4, H)] - (y[np.arange(H)[:, None], runs(q3, H)]))
    z = f64(gn) * (top + fy * (bot - top))
    out_0 = unpack_fp4(w4_words, w4_scales).T @ mxq(z, 0, "e4m3")
    return (out_0,) + planes(out_0)

from contextlib import ExitStack

import concourse.mybir as mybir
from concourse.masks import make_identity

FLOPS = 4 * 2 * 512 * 512 * 512

F32 = mybir.dt.float32
BF16 = mybir.dt.bfloat16
I32 = mybir.dt.int32
U32 = mybir.dt.uint32
U16 = mybir.dt.uint16
U8 = mybir.dt.uint8
FP8X4 = mybir.dt.float8_e4m3fn_x4
FP4X4 = mybir.dt.float4_e2m1fn_x4
MULT = mybir.AluOpType.mult
COPY = mybir.ActivationFunctionType.Copy
SIGMOID = mybir.ActivationFunctionType.Sigmoid

P = 128
PACK = 4
CELLS = 2048
S = 512
BLOCK = 128
STRIPE = 16
CHUNKS = ((0, 2, ((0, 1), (2, 3))), (2, 1, ((0, 1, 2, 3),)), (3, 1, ((0, 1, 2), (3,))))


def tile_picked_bilcomp_none_po_kernel(
    tc, x_words, x_scales, w1_words, w1_scales, w2_words, w2_scales, w3_words, w3_scales, gn,
    w4_words, w4_scales, offs, two, thr, q1, q2, q3, q4, out_0, out_1, out_2,
):
    nc = tc.nc
    with ExitStack() as ctx:
        keep = ctx.enter_context(tc.tile_pool(name="keep", bufs=1))
        ring = ctx.enter_context(tc.tile_pool(name="ring", bufs=2))
        psum = ctx.enter_context(tc.psum_pool(name="psum", bufs=2))

        def load_list(src, name):
            tile = keep.tile([P, S // STRIPE], U16, name=name)
            nc.sync.dma_start(tile[:], src)
            return tile

        def load_words(src, name):
            tile = keep.tile([P, 2 * S], U8, name=name, align_bytes=64)
            nc.sync.dma_start(tile[:].bitcast(I32), src[0].bitcast(I32))
            return tile

        def load_scales(dst, src):
            for quad in range(4):
                nc.sync.dma_start(
                    dst[32 * quad : 32 * quad + 4, :].bitcast(I32), src[0, 4 * quad : 4 * quad + 4, :].bitcast(I32)
                )

        def deal(words, scales, name):
            dealt_words = keep.tile([P, 2 * S], U8, name=name + "_words", align_bytes=64)
            dealt_scales = keep.tile([P, S], U8, name=name + "_scales", align_bytes=64)
            nc.vector.tensor_copy(
                dealt_words[:].rearrange("p (t m b) -> p t m b", t=PACK, b=2),
                words[:].rearrange("p (m t b) -> p t m b", t=PACK, b=2),
            )
            nc.vector.tensor_copy(
                dealt_scales[:].rearrange("p (t m) -> p t m", t=PACK),
                scales.rearrange("p (m t) -> p t m", t=PACK),
            )
            return dealt_words, dealt_scales

        def pick(offsets, name):
            words = keep.tile([P, S], U32, name=name + "_words", align_bytes=64)
            scales = keep.tile([P, S], U8, name=name + "_scales", align_bytes=64)
            nc.vector.tensor_copy(words[:], cell_words[:].indirect(offsets[:]))
            nc.vector.tensor_copy(scales[:], cell_scales[:].indirect(offsets[:]))
            return words, scales

        def project(out, weights, t, moving, cols):
            nc.tensor.matmul_mx(
                out,
                lhsT=weights[0][:, 2 * P * t : 2 * P * (t + 1)].bitcast(FP4X4),
                lhsT_scale=weights[1][:, P * t : P * (t + 1)],
                rhs=moving[0][:, cols].bitcast(FP8X4),
                rhs_scale=moving[1][:, cols],
                start=True,
                stop=True,
            )

        def add_turned(out, parts):
            for n, part in enumerate(parts):
                nc.tensor.matmul(
                    out, lhsT=part, rhs=ident[:], is_transpose=True, start=(n == 0), stop=(n == len(parts) - 1)
                )

        w_scales = keep.tile([P, 4 * S], U8, name="w_scales", align_bytes=64)
        cell_scales = keep.tile([P, CELLS], U8, name="cell_scales", align_bytes=64)
        nc.vector.memset(w_scales[:].bitcast(I32), 0)
        nc.vector.memset(cell_scales[:].bitcast(I32), 0)
        ident = keep.tile([P, P], F32, name="ident")
        make_identity(nc, ident[:])

        w2_raw = load_words(w2_words, "w2_raw")
        w1_raw = load_words(w1_words, "w1_raw")
        two_list = load_list(two, "two_list")
        cell_words = keep.tile([P, CELLS], U32, name="cell_words", align_bytes=64)
        nc.sync.dma_start(cell_words[:].bitcast(I32), x_words[0].rearrange("p c r -> p (c r)").bitcast(I32))
        load_scales(w_scales[:, S : 2 * S], w2_scales)
        load_scales(cell_scales[:], x_scales)
        offs_list = load_list(offs, "offs_list")
        load_scales(w_scales[:, 0:S], w1_scales)
        gain = keep.tile([P, PACK], F32, name="gain")
        nc.sync.dma_start(gain[:], gn.rearrange("(p t) o -> p (t o)", t=PACK))
        thr_list = load_list(thr, "thr_list")
        corner_lists = [load_list(q, "corner%d" % n) for n, q in enumerate((q1, q2, q3, q4))]
        w3_raw = load_words(w3_words, "w3_raw")
        load_scales(w_scales[:, 2 * S : 3 * S], w3_scales)
        w4_raw = load_words(w4_words, "w4_raw")
        load_scales(w_scales[:, 3 * S : 4 * S], w4_scales)

        w2_dealt = deal(w2_raw, w_scales[:, S : 2 * S], "w2")
        w1_dealt = deal(w1_raw, w_scales[:, 0:S], "w1")
        x_two = pick(two_list, "x_two")
        x_offs = pick(offs_list, "x_offs")
        minus_gain = keep.tile([P, PACK], F32, name="minus_gain")
        nc.gpsimd.tensor_scalar(minus_gain[:], gain[:], -1.0, 0.0, op0=MULT, op1=mybir.AluOpType.add)
        x_thr = pick(thr_list, "x_thr")
        w4_dealt = deal(w4_raw, w_scales[:, 3 * S : 4 * S], "w4")

        near, far, y_plus, y_minus = [], [], [], []
        for t in range(PACK):
            bank = psum.tile([P, S], F32, name="wide", bufs=4)
            project(bank[:], w2_dealt, t, x_two, slice(0, S))
            near.append(keep.tile([P, S], F32, name="near%d" % t))
            far.append(keep.tile([P, S], F32, name="far%d" % t))
            nc.scalar.activation(near[t][:], bank[:], SIGMOID, scale=-1.0)
            nc.scalar.activation(far[t][:], bank[:], SIGMOID)
            bank = psum.tile([P, S], F32, name="wide", bufs=4)
            project(bank[:], w1_dealt, t, x_offs, slice(0, S))
            y_minus.append(keep.tile([P, S], F32, name="y_minus%d" % t))
            y_plus.append(keep.tile([P, S], F32, name="y_plus%d" % t))
            nc.scalar.activation(y_minus[t][:], bank[:], COPY, scale=minus_gain[:, t : t + 1])
            nc.scalar.activation(y_plus[t][:], bank[:], COPY, scale=gain[:, t : t + 1])

        fy_turned = keep.tile([P, S // BLOCK, PACK, P], F32, name="fy_turned")
        for b in range(S // BLOCK):
            cols = slice(BLOCK * b, BLOCK * (b + 1))
            bank = psum.tile([P, S], F32, name="wide", bufs=4)
            nc.tensor.matmul_mx(
                bank[:],
                lhsT=x_thr[0][:, cols].bitcast(FP8X4),
                lhsT_scale=x_thr[1][:, cols],
                rhs=w3_raw[:].bitcast(FP4X4),
                rhs_scale=w_scales[:, 2 * S : 3 * S],
                start=True,
                stop=True,
            )
            nc.scalar.activation(fy_turned[:, b, :, :], bank[:].rearrange("j (p t) -> j t p", t=PACK), SIGMOID)

        z_words = keep.tile([P, S], U32, name="z_words", align_bytes=64)
        z_scales = keep.tile([P, S], U8, name="z_scales", align_bytes=64)
        out_words = keep.tile([P, S], U32, name="out_words", align_bytes=64)
        out_scales = keep.tile([P, S], U8, name="out_scales", align_bytes=64)
        out_rows = out_0.rearrange("(p t) j -> p t j", t=PACK)
        out_codes = out_1[0].rearrange("p c r -> p (c r)").bitcast(I32)

        def finish_block(b, z_bank):
            cols = slice(BLOCK * b, BLOCK * (b + 1))
            z_grouped = ring.tile([P, BLOCK, PACK], BF16, name="z_grouped", align_bytes=64)
            nc.scalar.copy(z_grouped[:], z_bank[:].rearrange("p (t j) -> p j t", t=PACK))
            nc.vector.quantize_mx(
                out=z_words[:, cols].bitcast(FP8X4),
                scales=z_scales[:, cols],
                in_=z_grouped[:].rearrange("p j t -> p (j t)"),
            )
            bank = psum.tile([P, S], F32, name="wide", bufs=4)
            for t in range(PACK):
                project(bank[:, BLOCK * t : BLOCK * (t + 1)], w4_dealt, t, (z_words, z_scales), cols)
            out_grouped = ring.tile([P, BLOCK, PACK], BF16, name="out_grouped", align_bytes=64)
            turned = bank[:].rearrange("p (t j) -> p j t", t=PACK)
            if b == S // BLOCK - 1:
                nc.vector.tensor_copy(out_grouped[:], turned)
            else:
                nc.scalar.copy(out_grouped[:], turned)
            result = ring.tile([P, PACK, BLOCK], F32, name="result")
            nc.scalar.copy(result[:].rearrange("p t j -> p (t j)"), bank[:])
            nc.sync.dma_start(out_rows[:, :, cols], result[:])
            nc.vector.quantize_mx(
                out=out_words[:, cols].bitcast(FP8X4),
                scales=out_scales[:, cols],
                in_=out_grouped[:].rearrange("p j t -> p (j t)"),
            )
            nc.sync.dma_start(out_codes[:, cols], out_words[:, cols].bitcast(I32))

        for first, blocks, groups in CHUNKS:
            width = BLOCK * blocks
            cols = slice(BLOCK * first, BLOCK * first + width)
            entries = slice(cols.start // STRIPE, cols.stop // STRIPE)
            z_banks = [psum.tile([P, S], F32, name="wide", bufs=4) for b in range(blocks)]
            for tiles in groups:
                used = P * blocks * len(tiles)
                top_bank = psum.tile([P, S], F32, name="top_bank")
                rise_bank = psum.tile([P, S], F32, name="rise_bank")
                for n, t in enumerate(tiles):
                    terms = ring.tile([P, 4, width], F32, name="terms", bufs=3)
                    factors = ((y_minus, near), (y_minus, far), (y_plus, near), (y_plus, far))
                    for c, (window, weight) in enumerate(factors):
                        nc.vector.tensor_tensor(
                            terms[:, c, :], window[t][:].indirect(corner_lists[c][:, entries]), weight[t][:, cols], MULT
                        )
                    for bank, count in ((top_bank, 2), (rise_bank, 4)):
                        for b in range(blocks):
                            place = P * (b * len(tiles) + n)
                            add_turned(
                                bank[:, place : place + P],
                                [terms[:, c, BLOCK * b : BLOCK * (b + 1)] for c in range(count)],
                            )
                top = ring.tile([P, S], F32, name="top")
                rise = ring.tile([P, S], F32, name="rise")
                nc.scalar.activation(top[:, 0:used], top_bank[:, 0:used], COPY, scale=-1.0)
                nc.vector.tensor_tensor(
                    rise[:, 0:used].rearrange("j (b t p) -> j b t p", b=blocks, p=P),
                    rise_bank[:, 0:used].rearrange("j (b t p) -> j b t p", b=blocks, p=P),
                    fy_turned[:, first : first + blocks, tiles[0] : tiles[-1] + 1, :],
                    MULT,
                )
                for b in range(blocks):
                    for n, t in enumerate(tiles):
                        place = slice(P * (b * len(tiles) + n), P * (b * len(tiles) + n + 1))
                        add_turned(z_banks[b][:, BLOCK * t : BLOCK * (t + 1)], [top[:, place], rise[:, place]])
            for b in range(blocks):
                finish_block(first + b, z_banks[b])

        for quad in range(4):
            queue = nc.sync if quad % 2 else nc.scalar
            queue.dma_start(
                out_2[0, 4 * quad : 4 * quad + 4, :].bitcast(I32), out_scales[32 * quad : 32 * quad + 4, :].bitcast(I32)
            )
